import numpy as np
CORES = [14,30,46,142,158,174,270,286,302,398,414,430]
N = 12
T, M = 2048, 128
def entries(a): return a.T.reshape(-1)
def pack(v, P): return np.ascontiguousarray(np.asarray(v, np.int32).reshape(-1, P).T)
def lists(rng, how):
    I = rng.integers(0, T, (N, M))
    if how == "alike": I[:] = rng.integers(0, T, (N, 1))
    if how == "distinct": I = np.stack([rng.permutation(T)[:M] for r in range(N)])
    if how == "sorted": I = np.sort(I, axis=1)
    if how == "edge": I = np.where(rng.random((N, M)) < 0.5, 0, T - 1)
    return {"idx": np.stack([pack(I[r], 16) for r in range(N)])}
def setup_inputs(rng):
    return dict({"x": rng.standard_normal((N, 128, T), dtype=np.float32)}, **lists(rng, "uniform"))
def setup_inputs_alike(rng):
    d = setup_inputs(rng); d.update(lists(rng, "alike"))
    for k in ("x",): d[k] = (d[k].astype(np.float32) * 1024.0).astype(d[k].dtype)
    return d
def setup_inputs_distinct(rng):
    d = setup_inputs(rng); d.update(lists(rng, "distinct"))
    for k in ("x",): d[k] = (d[k].astype(np.float32) * (1 / 1024.0)).astype(d[k].dtype)
    return d
def setup_inputs_edge(rng):
    d = setup_inputs(rng); d.update(lists(rng, "edge"))
    return d
def setup_inputs_sorted(rng):
    d = setup_inputs(rng); d.update(lists(rng, "sorted"))
    return d
def check_inputs(x):
    bad = []
    if x["idx"].min() < 0 or x["idx"].max() >= T: bad.append("idx out of range")
    return bad
def reference(x, idx):
    s = sum(x[r].astype(np.float64)[:, entries(idx[r])] for r in range(N)).astype(np.float32)
    return {"y": np.broadcast_to(s, (N, 128, M))}

@@ -1,0 +1,114 @@
+from concourse.bass import DstId, RemoteDMATransfer
+from concourse.mybir import AluOpType
+
+M = 128
+TCOLS = 2048
+NSLOT = 6
+NPART = 3
+
+SCRATCH = {
+    "xs": ("sbuf", [128, TCOLS], "float32"),
+    "idx32": ("sbuf", [128, 8], "int32"),
+    "off": ("sbuf", [128, 8], "uint16"),
+    "part": ("sbuf", [128, NPART * M], "float32"),
+    "land": ("sbuf", [128, NSLOT * M], "float32"),
+    "acc": ("psum", [128, M], "float32"),
+}
+SEMAPHORES = ["ldx", "ldi", "vs", "sent", "st", "arr0", "arr1", "arr2"]
+
+
+def plan(cores, topo):
+    n = len(cores)
+    twin, ring = {}, {}
+    for r, c in enumerate(cores):
+        mine = topo.rack(topo.host(c))
+        twin[r] = [s for s, d in enumerate(cores)
+                   if topo.rack(topo.host(d)) != mine and topo.may_write(c, d) and topo.chip(d) == topo.chip(c)][0]
+        near = [s for s, d in enumerate(cores) if s == r or topo.same_plane(c, d)]
+        i = near.index(r)
+        ring[r] = [near[(i + k) % len(near)] for k in range(1, len(near))]
+    calls = [
+        {r: [twin[r]] for r in range(n)},
+        {r: ring[r][:-1] for r in range(n)},
+        {r: ring[r][-1:] for r in range(n)},
+    ]
+    return calls, [0, 1, 1]
+
+
+def rank_program(g, core, T, topo):
+    rank = T.rank_of(core)
+    if rank is None:
+        return
+    cores = list(T.cores)
+    calls, hop_of = plan(cores, topo)
+    sem = T.sem
+    v = g.vector
+
+    slot, nxt = {}, {d: 0 for d in range(len(cores))}
+    for k, call in enumerate(calls):
+        for pos in range(max(len(x) for x in call.values())):
+            for s in range(len(cores)):
+                if pos < len(call[s]):
+                    d = call[s][pos]
+                    slot[(k, s, d)] = nxt[d]
+                    nxt[d] += 1
+
+    def part(h):
+        return T.part[:, h * M:(h + 1) * M]
+
+    def land(i):
+        return T.land[:, i * M:(i + 1) * M]
+
+    g.sync.dma_start(T.xs[:], T.x[:]).then_inc(sem.ldx, 16)
+    for k in range(8):
+        g.scalar.dma_start(T.idx32[16 * k:16 * k + 16, :], T.idx[:]).then_inc(sem.ldi, 16)
+
+    nv = [0]
+
+    def vdone(ins):
+        ins.then_inc(sem.vs, 1)
+        nv[0] += 1
+
+    v.wait_ge(sem.ldi, 128)
+    vdone(v.tensor_copy(T.off[:], T.idx32[:]))
+    v.wait_ge(sem.vs, nv[0])
+    v.wait_ge(sem.ldx, 16)
+    vdone(v.tensor_copy(part(0), T.xs[:, 0:TCOLS].indirect(T.off[:, 0:8])))
+
+    sent = 0
+    nhops = max(hop_of) + 1
+    for h in range(nhops):
+        ks = [k for k in range(len(calls)) if hop_of[k] == h]
+        g.wait_ge(sem.vs, nv[0])
+        for k in ks:
+            dsts = calls[k][rank]
+            mask = topo.mask(core, cores[dsts[0]])
+            for d in dsts:
+                mask &= topo.mask(core, cores[d])
+            ids = []
+            for d in dsts:
+                rid, pid = topo.addr(cores[d], core)
+                ids.append(DstId(rid=rid, pnc=pid))
+            g.remote_dma_fused([RemoteDMATransfer(
+                dst_ids=ids, dma_engine_mask=mask, remote_sem=sem["arr%d" % k],
+                srcs=[part(h)], dsts=[land(slot[(k, rank, d)]) for d in dsts], alu_op=0)], local_sem=sem.sent)
+            sent += bin(mask).count("1")
+        v.wait_ge(sem.vs, nv[0])
+        vdone(v.tensor_copy(T.acc[:], part(h)))
+        todo = []
+        for k in ks:
+            froms = [s for s in range(len(cores)) if rank in calls[k][s]]
+            todo.append((k, froms))
+        for j, (k, froms) in enumerate(todo):
+            inc = sum(bin(topo.mask(cores[s], core)).count("1") for s in froms)
+            v.wait_ge(sem["arr%d" % k], inc)
+            for i, s in enumerate(froms):
+                last = j == len(todo) - 1 and i == len(froms) - 1
+                v.wait_ge(sem.vs, nv[0])
+                out = part(h + 1) if last else T.acc[:]
+                vdone(v.tensor_tensor(out, land(slot[(k, s, rank)]), T.acc[:], AluOpType.add))
+
+    g.sync.wait_ge(sem.vs, nv[0])
+    g.sync.dma_start(T.y[:], part(nhops)).then_inc(sem.st, 16)
+    g.sync.wait_ge(sem.st, 16)
+    g.wait_ge(sem.sent, sent)

@@ -3,36 +3,47 @@ from concourse.mybir import AluOpType
 
 M = 128
 TCOLS = 2048
-NSLOT = 6
-NPART = 3
+W = 44
+LO = [0, 44, 84]
 
 SCRATCH = {
     "xs": ("sbuf", [128, TCOLS], "float32"),
     "idx32": ("sbuf", [128, 8], "int32"),
+    "idxf": ("sbuf", [128, 8], "float32"),
+    "ones": ("sbuf", [128, 128], "float32"),
+    "rep": ("sbuf", [128, 128], "float32"),
     "off": ("sbuf", [128, 8], "uint16"),
-    "part": ("sbuf", [128, NPART * M], "float32"),
-    "land": ("sbuf", [128, NSLOT * M], "float32"),
-    "acc": ("psum", [128, M], "float32"),
+    "gat": ("sbuf", [128, M], "float32"),
+    "hs": ("sbuf", [128, 2 * W], "float32"),
+    "l1": ("sbuf", [128, 2 * W], "float32"),
+    "l2": ("sbuf", [128, W], "float32"),
+    "la": ("sbuf", [128, 3 * W], "float32"),
+    "lb": ("sbuf", [128, 3 * W], "float32"),
+    "ys": ("sbuf", [128, M], "float32"),
+    "pidx": ("psum", [128, 512], "float32"),
+    "acc": ("psum", [128, 512], "float32"),
 }
-SEMAPHORES = ["ldx", "ldi", "vs", "sent", "st", "arr0", "arr1", "arr2"]
+SEMAPHORES = ["ldx", "ldi", "vs", "gr", "tm", "sent", "st", "arr1", "arr2", "arr3", "arr4"]
+
+
+def bits(mask):
+    return [1 << i for i in range(mask.bit_length()) if mask >> i & 1]
 
 
 def plan(cores, topo):
     n = len(cores)
-    twin, ring = {}, {}
+    pos, others, twin, ring = {}, {}, {}, {}
     for r, c in enumerate(cores):
+        home = [s for s, d in enumerate(cores) if topo.host(d) == topo.host(c)]
+        pos[r] = home.index(r)
+        others[r] = [s for s in home if s != r]
         mine = topo.rack(topo.host(c))
         twin[r] = [s for s, d in enumerate(cores)
                    if topo.rack(topo.host(d)) != mine and topo.may_write(c, d) and topo.chip(d) == topo.chip(c)][0]
         near = [s for s, d in enumerate(cores) if s == r or topo.same_plane(c, d)]
         i = near.index(r)
         ring[r] = [near[(i + k) % len(near)] for k in range(1, len(near))]
-    calls = [
-        {r: [twin[r]] for r in range(n)},
-        {r: ring[r][:-1] for r in range(n)},
-        {r: ring[r][-1:] for r in range(n)},
-    ]
-    return calls, [0, 1, 1]
+    return pos, others, twin, ring
 
 
 def rank_program(g, core, T, topo):
@@ -40,75 +51,118 @@ def rank_program(g, core, T, topo):
     if rank is None:
         return
     cores = list(T.cores)
-    calls, hop_of = plan(cores, topo)
+    pos, others, twin, ring = plan(cores, topo)
     sem = T.sem
     v = g.vector
+    a = pos[rank]
 
-    slot, nxt = {}, {d: 0 for d in range(len(cores))}
-    for k, call in enumerate(calls):
-        for pos in range(max(len(x) for x in call.values())):
-            for s in range(len(cores)):
-                if pos < len(call[s]):
-                    d = call[s][pos]
-                    slot[(k, s, d)] = nxt[d]
-                    nxt[d] += 1
+    def dst_id(d):
+        rid, pid = topo.addr(cores[d], core)
+        return DstId(rid=rid, pnc=pid)
 
-    def part(h):
-        return T.part[:, h * M:(h + 1) * M]
+    def piece(buf, k):
+        return buf[:, k * W:(k + 1) * W]
 
-    def land(i):
-        return T.land[:, i * M:(i + 1) * M]
+    def hop1_mask(s, d):
+        b = bits(topo.mask(cores[s], cores[others[s][0]]) & topo.mask(cores[s], cores[others[s][1]]))
+        n = len(b) // 2
+        j = others[s].index(d)
+        return sum(b[j * n:(j + 1) * n])
 
-    g.sync.dma_start(T.xs[:], T.x[:]).then_inc(sem.ldx, 16)
-    for k in range(8):
-        g.scalar.dma_start(T.idx32[16 * k:16 * k + 16, :], T.idx[:]).then_inc(sem.ldi, 16)
+    def count(mask):
+        return len(bits(mask))
 
     nv = [0]
 
-    def vdone(ins):
+    def vdo(ins):
         ins.then_inc(sem.vs, 1)
         nv[0] += 1
 
-    v.wait_ge(sem.ldi, 128)
-    vdone(v.tensor_copy(T.off[:], T.idx32[:]))
-    v.wait_ge(sem.vs, nv[0])
+    def vsync():
+        v.wait_ge(sem.vs, nv[0])
+
+    g.sync.dma_start(T.xs[:], T.x[:]).then_inc(sem.ldx, 16)
+    g.scalar.dma_start(T.idx32[0:16, :], T.idx[:]).then_inc(sem.ldi, 16)
+    vdo(v.memset(T.ones[0:16, :], 1.0))
+    g.wait_ge(sem.vs, nv[0])
+    g.affine_select(T.rep[0:16, :], T.ones[0:16, :], [[0, 8], [-1, 16]], AluOpType.is_equal, 0.0, 0, 1).then_inc(sem.gr, 1)
+    vsync()
+    v.wait_ge(sem.ldi, 16)
+    vdo(v.tensor_copy(T.idxf[0:16, :], T.idx32[0:16, :]))
+    g.tensor.wait_ge(sem.gr, 1)
+    g.tensor.wait_ge(sem.vs, nv[0])
+    g.tensor.matmul(T.pidx[:, 0:8], T.rep[0:16, :], T.idxf[0:16, :], True, True).then_inc(sem.tm, 1)
+    vsync()
+    v.wait_ge(sem.tm, 1)
+    vdo(v.tensor_copy(T.off[:], T.pidx[:, 0:8]))
+
+    vsync()
     v.wait_ge(sem.ldx, 16)
-    vdone(v.tensor_copy(part(0), T.xs[:, 0:TCOLS].indirect(T.off[:, 0:8])))
+    vdo(v.tensor_copy(T.gat[:], T.xs[:, 0:TCOLS].indirect(T.off[:, 0:8])))
 
     sent = 0
-    nhops = max(hop_of) + 1
-    for h in range(nhops):
-        ks = [k for k in range(len(calls)) if hop_of[k] == h]
-        g.wait_ge(sem.vs, nv[0])
-        for k in ks:
-            dsts = calls[k][rank]
-            mask = topo.mask(core, cores[dsts[0]])
-            for d in dsts:
-                mask &= topo.mask(core, cores[d])
-            ids = []
-            for d in dsts:
-                rid, pid = topo.addr(cores[d], core)
-                ids.append(DstId(rid=rid, pnc=pid))
-            g.remote_dma_fused([RemoteDMATransfer(
-                dst_ids=ids, dma_engine_mask=mask, remote_sem=sem["arr%d" % k],
-                srcs=[part(h)], dsts=[land(slot[(k, rank, d)]) for d in dsts], alu_op=0)], local_sem=sem.sent)
-            sent += bin(mask).count("1")
-        v.wait_ge(sem.vs, nv[0])
-        vdone(v.tensor_copy(T.acc[:], part(h)))
-        todo = []
-        for k in ks:
-            froms = [s for s in range(len(cores)) if rank in calls[k][s]]
-            todo.append((k, froms))
-        for j, (k, froms) in enumerate(todo):
-            inc = sum(bin(topo.mask(cores[s], core)).count("1") for s in froms)
-            v.wait_ge(sem["arr%d" % k], inc)
-            for i, s in enumerate(froms):
-                last = j == len(todo) - 1 and i == len(froms) - 1
-                v.wait_ge(sem.vs, nv[0])
-                out = part(h + 1) if last else T.acc[:]
-                vdone(v.tensor_tensor(out, land(slot[(k, s, rank)]), T.acc[:], AluOpType.add))
+    acc = T.acc[:, 0:W]
+
+    g.wait_ge(sem.vs, nv[0])
+    trs = []
+    for d in others[rank]:
+        m = hop1_mask(rank, d)
+        trs.append(RemoteDMATransfer(
+            dst_ids=[dst_id(d)], dma_engine_mask=m, remote_sem=sem.arr1,
+            srcs=[T.gat[:, LO[pos[d]]:LO[pos[d]] + W]], dsts=[piece(T.l1, others[d].index(rank))], alu_op=0))
+        sent += count(m)
+    g.remote_dma_fused(trs, local_sem=sem.sent)
+
+    v.wait_ge(sem.arr1, sum(count(hop1_mask(s, rank)) for s in others[rank]))
+    vsync()
+    vdo(v.tensor_tensor(acc, T.gat[:, LO[a]:LO[a] + W], piece(T.l1, 0), AluOpType.add))
+    vsync()
+    vdo(v.tensor_tensor(piece(T.hs, 0), piece(T.l1, 1), acc, AluOpType.add))
+
+    g.wait_ge(sem.vs, nv[0])
+    m = topo.mask(core, cores[twin[rank]])
+    g.remote_dma_fused([RemoteDMATransfer(
+        dst_ids=[dst_id(twin[rank])], dma_engine_mask=m, remote_sem=sem.arr2,
+        srcs=[piece(T.hs, 0)], dsts=[T.l2[:]], alu_op=0)], local_sem=sem.sent)
+    sent += count(m)
+
+    vsync()
+    vdo(v.tensor_copy(acc, piece(T.hs, 0)))
+    v.wait_ge(sem.arr2, count(topo.mask(cores[twin[rank]], core)))
+    vsync()
+    vdo(v.tensor_tensor(piece(T.hs, 1), T.l2[:], acc, AluOpType.add))
+
+    g.wait_ge(sem.vs, nv[0])
+    for dsts, s3 in ((ring[rank][:-1], sem.arr3), (ring[rank][-1:], sem.arr4)):
+        m = topo.mask(core, cores[dsts[0]])
+        for d in dsts:
+            m &= topo.mask(core, cores[d])
+        lands = [piece(T.la if topo.host(cores[d]) == topo.host(core) else T.lb, a) for d in dsts]
+        g.remote_dma_fused([RemoteDMATransfer(
+            dst_ids=[dst_id(d) for d in dsts], dma_engine_mask=m, remote_sem=s3,
+            srcs=[piece(T.hs, 1)], dsts=lands, alu_op=0)], local_sem=sem.sent)
+        sent += count(m)
+
+    vsync()
+    vdo(v.tensor_copy(acc, piece(T.hs, 1)))
+
+    late = [s for s in ring[rank] if ring[s][-1] == rank][0]
+    early = [s for s in ring[rank] if s != late]
+
+    def total(k):
+        skip = 0 if k == 0 else LO[k - 1] + W - LO[k]
+        own = T.acc[:, skip:W] if k == a else T.la[:, k * W + skip:(k + 1) * W]
+        vsync()
+        vdo(v.tensor_tensor(T.ys[:, LO[k] + skip:LO[k] + W], T.lb[:, k * W + skip:(k + 1) * W], own, AluOpType.add))
+
+    v.wait_ge(sem.arr3, sum(count(topo.mask(cores[s], core)) for s in early))
+    for k in range(len(LO)):
+        if k != pos[late]:
+            total(k)
+    v.wait_ge(sem.arr4, count(topo.mask(cores[late], core)))
+    total(pos[late])
 
     g.sync.wait_ge(sem.vs, nv[0])
-    g.sync.dma_start(T.y[:], part(nhops)).then_inc(sem.st, 16)
+    g.sync.dma_start(T.y[:], T.ys[:]).then_inc(sem.st, 16)
     g.sync.wait_ge(sem.st, 16)
     g.wait_ge(sem.sent, sent)

@@ -1,10 +1,13 @@
 from concourse.bass import DstId, RemoteDMATransfer
-from concourse.mybir import AluOpType
+from concourse.mybir import AluOpType, ActivationFunctionType
 
 M = 128
 TCOLS = 2048
-W = 44
-LO = [0, 44, 84]
+LO = [0, 44, 88]
+WID = [44, 44, 40]
+WMAX = 44
+B = 32
+OC = 2
 
 SCRATCH = {
     "xs": ("sbuf", [128, TCOLS], "float32"),
@@ -14,16 +17,16 @@ SCRATCH = {
     "rep": ("sbuf", [128, 128], "float32"),
     "off": ("sbuf", [128, 8], "uint16"),
     "gat": ("sbuf", [128, M], "float32"),
-    "hs": ("sbuf", [128, 2 * W], "float32"),
-    "l1": ("sbuf", [128, 2 * W], "float32"),
-    "l2": ("sbuf", [128, W], "float32"),
-    "la": ("sbuf", [128, 3 * W], "float32"),
-    "lb": ("sbuf", [128, 3 * W], "float32"),
+    "l1": ("sbuf", [128, 5 * WMAX], "float32"),
+    "hs": ("sbuf", [128, WMAX], "float32"),
+    "l2": ("sbuf", [128, WMAX], "float32"),
     "ys": ("sbuf", [128, M], "float32"),
     "pidx": ("psum", [128, 512], "float32"),
     "acc": ("psum", [128, 512], "float32"),
 }
-SEMAPHORES = ["ldx", "ldi", "vs", "gr", "tm", "sent", "st", "arr1", "arr2", "arr3", "arr4"]
+SEMAPHORES = (["ldx", "ldi", "vs", "sg1", "sg2", "gr", "tm", "sent", "st", "st2", "arr2"]
+              + ["a1_%d_%d" % (gi, hb) for gi in range(3) for hb in range(2)]
+              + ["a3_%d" % p for p in range(3)])
 
 
 def bits(mask):
@@ -31,19 +34,30 @@ def bits(mask):
 
 
 def plan(cores, topo):
-    n = len(cores)
-    pos, others, twin, ring = {}, {}, {}, {}
+    pos, hb, others, twin, near, sched = {}, {}, {}, {}, {}, {}
     for r, c in enumerate(cores):
         home = [s for s, d in enumerate(cores) if topo.host(d) == topo.host(c)]
-        pos[r] = home.index(r)
-        others[r] = [s for s in home if s != r]
+        p = home.index(r)
+        pos[r] = p
+        others[r] = [home[(p + k) % len(home)] for k in range(1, len(home))]
         mine = topo.rack(topo.host(c))
         twin[r] = [s for s, d in enumerate(cores)
                    if topo.rack(topo.host(d)) != mine and topo.may_write(c, d) and topo.chip(d) == topo.chip(c)][0]
-        near = [s for s, d in enumerate(cores) if s == r or topo.same_plane(c, d)]
-        i = near.index(r)
-        ring[r] = [near[(i + k) % len(near)] for k in range(1, len(near))]
-    return pos, others, twin, ring
+        near[r] = [s for s, d in enumerate(cores) if s == r or topo.same_plane(c, d)]
+        hb[r] = sorted({topo.host(cores[s]) for s in near[r]}).index(topo.host(c))
+    for r in range(len(cores)):
+        n = len(near[r])
+        i = near[r].index(r)
+        groups = []
+        for o in range(1, n):
+            d = near[r][(i + o) % n]
+            hit = [gk for gk in groups if gk[0] == pos[d]]
+            if hit:
+                hit[0][1].append(d)
+            else:
+                groups.append((pos[d], [d]))
+        sched[r] = groups
+    return pos, hb, others, twin, near, sched
 
 
 def rank_program(g, core, T, topo):
@@ -51,26 +65,36 @@ def rank_program(g, core, T, topo):
     if rank is None:
         return
     cores = list(T.cores)
-    pos, others, twin, ring = plan(cores, topo)
+    pos, hb, others, twin, near, sched = plan(cores, topo)
     sem = T.sem
     v = g.vector
     a = pos[rank]
+    w = WID[a]
 
     def dst_id(d):
         rid, pid = topo.addr(cores[d], core)
         return DstId(rid=rid, pnc=pid)
 
-    def piece(buf, k):
-        return buf[:, k * W:(k + 1) * W]
-
-    def hop1_mask(s, d):
-        b = bits(topo.mask(cores[s], cores[others[s][0]]) & topo.mask(cores[s], cores[others[s][1]]))
-        n = len(b) // 2
-        j = others[s].index(d)
-        return sum(b[j * n:(j + 1) * n])
-
     def count(mask):
         return len(bits(mask))
+
+    def common_mask(s, dsts):
+        m = topo.mask(cores[s], cores[dsts[0]])
+        for d in dsts:
+            m &= topo.mask(cores[s], cores[d])
+        return m
+
+    def place(s, d):
+        t = 0
+        for gi, (k, dsts) in enumerate(sched[s]):
+            for e in dsts:
+                if e == d:
+                    return gi, t
+                t += 1
+        return None
+
+    def cols(buf, k):
+        return buf[:, LO[k]:LO[k] + WID[k]]
 
     nv = [0]
 
@@ -96,73 +120,93 @@ def rank_program(g, core, T, topo):
     v.wait_ge(sem.tm, 1)
     vdo(v.tensor_copy(T.off[:], T.pidx[:, 0:8]))
 
-    vsync()
+    k1 = sched[rank][0][0]
+    lot1 = list(range(LO[k1] // B, (LO[k1] + WID[k1] + B - 1) // B))
+    lot2 = [b for b in range(M // B) if b not in lot1]
+
+    def halves(lot):
+        h = (len(lot) + 1) // 2
+        return lot[:h], lot[h:]
+
+    def take(lot):
+        b0, b1 = lot[0], lot[-1] + 1
+        return T.gat[:, b0 * B:b1 * B], T.xs[:, 0:TCOLS].indirect(T.off[:, b0 * OC:b1 * OC])
+
+    g.scalar.wait_ge(sem.vs, nv[0])
+    g.scalar.wait_ge(sem.ldx, 16)
     v.wait_ge(sem.ldx, 16)
-    vdo(v.tensor_copy(T.gat[:], T.xs[:, 0:TCOLS].indirect(T.off[:, 0:8])))
+    ready = []
+    for lot, ss in ((lot1, sem.sg1), (lot2, sem.sg2)):
+        lv, ls = halves(lot)
+        o, i = take(ls)
+        g.scalar.activation(o, i, ActivationFunctionType.Copy).then_inc(ss, 1)
+        o, i = take(lv)
+        vsync()
+        vdo(v.tensor_copy(o, i))
+        ready.append((nv[0], ss))
 
     sent = 0
-    acc = T.acc[:, 0:W]
 
-    g.wait_ge(sem.vs, nv[0])
-    trs = []
-    for d in others[rank]:
-        m = hop1_mask(rank, d)
-        trs.append(RemoteDMATransfer(
-            dst_ids=[dst_id(d)], dma_engine_mask=m, remote_sem=sem.arr1,
-            srcs=[T.gat[:, LO[pos[d]]:LO[pos[d]] + W]], dsts=[piece(T.l1, others[d].index(rank))], alu_op=0))
+    for gi, (k, dsts) in enumerate(sched[rank]):
+        if gi < len(ready):
+            g.wait_ge(sem.vs, ready[gi][0])
+            g.wait_ge(ready[gi][1], 1)
+        m = common_mask(rank, dsts)
+        lands = []
+        for d in dsts:
+            t = place(rank, d)[1]
+            lands.append(T.l1[:, t * WMAX:t * WMAX + WID[k]])
+        g.remote_dma_fused([RemoteDMATransfer(
+            dst_ids=[dst_id(d) for d in dsts], dma_engine_mask=m, remote_sem=sem["a1_%d_%d" % (gi, hb[rank])],
+            srcs=[cols(T.gat, k)], dsts=lands, alu_op=0)], local_sem=sem.sent)
         sent += count(m)
-    g.remote_dma_fused(trs, local_sem=sem.sent)
 
-    v.wait_ge(sem.arr1, sum(count(hop1_mask(s, rank)) for s in others[rank]))
-    vsync()
-    vdo(v.tensor_tensor(acc, T.gat[:, LO[a]:LO[a] + W], piece(T.l1, 0), AluOpType.add))
-    vsync()
-    vdo(v.tensor_tensor(piece(T.hs, 0), piece(T.l1, 1), acc, AluOpType.add))
+    acc = T.acc[:, 0:w]
+    inc = []
+    for s in near[rank]:
+        if s != rank:
+            gi, t = place(s, rank)
+            inc.append((t, gi, s))
+    inc.sort()
+    v.wait_ge(sem.sg1, 1)
+    v.wait_ge(sem.sg2, 1)
+    for n, (t, gi, s) in enumerate(inc):
+        v.wait_ge(sem["a1_%d_%d" % (gi, hb[s])], count(common_mask(s, sched[s][gi][1])))
+        land = T.l1[:, t * WMAX:t * WMAX + w]
+        prev = cols(T.gat, a) if n == 0 else acc
+        out = T.hs[:, 0:w] if n == len(inc) - 1 else acc
+        vsync()
+        vdo(v.tensor_tensor(out, land, prev, AluOpType.add))
 
     g.wait_ge(sem.vs, nv[0])
     m = topo.mask(core, cores[twin[rank]])
     g.remote_dma_fused([RemoteDMATransfer(
         dst_ids=[dst_id(twin[rank])], dma_engine_mask=m, remote_sem=sem.arr2,
-        srcs=[piece(T.hs, 0)], dsts=[T.l2[:]], alu_op=0)], local_sem=sem.sent)
+        srcs=[T.hs[:, 0:w]], dsts=[T.l2[:, 0:w]], alu_op=0)], local_sem=sem.sent)
     sent += count(m)
 
     vsync()
-    vdo(v.tensor_copy(acc, piece(T.hs, 0)))
+    vdo(v.tensor_copy(acc, T.hs[:, 0:w]))
     v.wait_ge(sem.arr2, count(topo.mask(cores[twin[rank]], core)))
     vsync()
-    vdo(v.tensor_tensor(piece(T.hs, 1), T.l2[:], acc, AluOpType.add))
+    vdo(v.tensor_tensor(cols(T.ys, a), T.l2[:, 0:w], acc, AluOpType.add))
 
     g.wait_ge(sem.vs, nv[0])
-    for dsts, s3 in ((ring[rank][:-1], sem.arr3), (ring[rank][-1:], sem.arr4)):
-        m = topo.mask(core, cores[dsts[0]])
-        for d in dsts:
-            m &= topo.mask(core, cores[d])
-        lands = [piece(T.la if topo.host(cores[d]) == topo.host(core) else T.lb, a) for d in dsts]
-        g.remote_dma_fused([RemoteDMATransfer(
-            dst_ids=[dst_id(d) for d in dsts], dma_engine_mask=m, remote_sem=s3,
-            srcs=[piece(T.hs, 1)], dsts=lands, alu_op=0)], local_sem=sem.sent)
-        sent += count(m)
+    m = common_mask(rank, others[rank])
+    g.remote_dma_fused([RemoteDMATransfer(
+        dst_ids=[dst_id(d) for d in others[rank]], dma_engine_mask=m, remote_sem=sem["a3_%d" % a],
+        srcs=[cols(T.ys, a)], dsts=[cols(T.ys, a) for d in others[rank]], alu_op=0)],
+        local_sem=sem.sent)
+    sent += count(m)
 
-    vsync()
-    vdo(v.tensor_copy(acc, piece(T.hs, 1)))
-
-    late = [s for s in ring[rank] if ring[s][-1] == rank][0]
-    early = [s for s in ring[rank] if s != late]
-
-    def total(k):
-        skip = 0 if k == 0 else LO[k - 1] + W - LO[k]
-        own = T.acc[:, skip:W] if k == a else T.la[:, k * W + skip:(k + 1) * W]
-        vsync()
-        vdo(v.tensor_tensor(T.ys[:, LO[k] + skip:LO[k] + W], T.lb[:, k * W + skip:(k + 1) * W], own, AluOpType.add))
-
-    v.wait_ge(sem.arr3, sum(count(topo.mask(cores[s], core)) for s in early))
-    for k in range(len(LO)):
-        if k != pos[late]:
-            total(k)
-    v.wait_ge(sem.arr4, count(topo.mask(cores[late], core)))
-    total(pos[late])
-
-    g.sync.wait_ge(sem.vs, nv[0])
-    g.sync.dma_start(T.y[:], T.ys[:]).then_inc(sem.st, 16)
+    early = [s for s in others[rank] if others[s][0] == rank][0]
+    late = [s for s in others[rank] if others[s][-1] == rank][0]
+    g.scalar.wait_ge(sem.vs, nv[0])
+    g.scalar.dma_start(cols(T.y, a), cols(T.ys, a)).then_inc(sem.st2, 16)
+    g.scalar.wait_ge(sem["a3_%d" % pos[early]], count(common_mask(early, others[early])))
+    g.scalar.dma_start(cols(T.y, pos[early]), cols(T.ys, pos[early])).then_inc(sem.st2, 16)
+    g.sync.wait_ge(sem["a3_%d" % pos[late]], count(common_mask(late, others[late])))
+    g.sync.dma_start(cols(T.y, pos[late]), cols(T.ys, pos[late])).then_inc(sem.st, 16)
     g.sync.wait_ge(sem.st, 16)
+    g.scalar.wait_ge(sem.st2, 32)
     g.wait_ge(sem.sent, sent)

from concourse.bass import DstId, RemoteDMATransfer
from concourse.mybir import AluOpType, ActivationFunctionType

M = 128
TCOLS = 2048
LO = [0, 44, 88]
WID = [44, 44, 40]
WMAX = 44
B = 32
OC = 2

SCRATCH = {
    "xs": ("sbuf", [128, TCOLS], "float32"),
    "idx32": ("sbuf", [128, 8], "int32"),
    "idxf": ("sbuf", [128, 8], "float32"),
    "ones": ("sbuf", [128, 128], "float32"),
    "rep": ("sbuf", [128, 128], "float32"),
    "off": ("sbuf", [128, 8], "uint16"),
    "gat": ("sbuf", [128, M], "float32"),
    "l1": ("sbuf", [128, 5 * WMAX], "float32"),
    "hs": ("sbuf", [128, WMAX], "float32"),
    "l2": ("sbuf", [128, WMAX], "float32"),
    "ys": ("sbuf", [128, M], "float32"),
    "pidx": ("psum", [128, 512], "float32"),
    "acc": ("psum", [128, 512], "float32"),
}
SEMAPHORES = (["ldx", "ldi", "vs", "sg1", "sg2", "gr", "tm", "sent", "st", "st2", "arr2"]
              + ["a1_%d_%d" % (gi, hb) for gi in range(3) for hb in range(2)]
              + ["a3_%d" % p for p in range(3)])


def bits(mask):
    return [1 << i for i in range(mask.bit_length()) if mask >> i & 1]


def plan(cores, topo):
    pos, hb, others, twin, near, sched = {}, {}, {}, {}, {}, {}
    for r, c in enumerate(cores):
        home = [s for s, d in enumerate(cores) if topo.host(d) == topo.host(c)]
        p = home.index(r)
        pos[r] = p
        others[r] = [home[(p + k) % len(home)] for k in range(1, len(home))]
        mine = topo.rack(topo.host(c))
        twin[r] = [s for s, d in enumerate(cores)
                   if topo.rack(topo.host(d)) != mine and topo.may_write(c, d) and topo.chip(d) == topo.chip(c)][0]
        near[r] = [s for s, d in enumerate(cores) if s == r or topo.same_plane(c, d)]
        hb[r] = sorted({topo.host(cores[s]) for s in near[r]}).index(topo.host(c))
    for r in range(len(cores)):
        n = len(near[r])
        i = near[r].index(r)
        groups = []
        for o in range(1, n):
            d = near[r][(i + o) % n]
            hit = [gk for gk in groups if gk[0] == pos[d]]
            if hit:
                hit[0][1].append(d)
            else:
                groups.append((pos[d], [d]))
        sched[r] = groups
    return pos, hb, others, twin, near, sched


def rank_program(g, core, T, topo):
    rank = T.rank_of(core)
    if rank is None:
        return
    cores = list(T.cores)
    pos, hb, others, twin, near, sched = plan(cores, topo)
    sem = T.sem
    v = g.vector
    a = pos[rank]
    w = WID[a]

    def dst_id(d):
        rid, pid = topo.addr(cores[d], core)
        return DstId(rid=rid, pnc=pid)

    def count(mask):
        return len(bits(mask))

    def common_mask(s, dsts):
        m = topo.mask(cores[s], cores[dsts[0]])
        for d in dsts:
            m &= topo.mask(cores[s], cores[d])
        return m

    def place(s, d):
        t = 0
        for gi, (k, dsts) in enumerate(sched[s]):
            for e in dsts:
                if e == d:
                    return gi, t
                t += 1
        return None

    def cols(buf, k):
        return buf[:, LO[k]:LO[k] + WID[k]]

    nv = [0]

    def vdo(ins):
        ins.then_inc(sem.vs, 1)
        nv[0] += 1

    def vsync():
        v.wait_ge(sem.vs, nv[0])

    g.sync.dma_start(T.xs[:], T.x[:]).then_inc(sem.ldx, 16)
    g.scalar.dma_start(T.idx32[0:16, :], T.idx[:]).then_inc(sem.ldi, 16)
    vdo(v.memset(T.ones[0:16, :], 1.0))
    g.wait_ge(sem.vs, nv[0])
    g.affine_select(T.rep[0:16, :], T.ones[0:16, :], [[0, 8], [-1, 16]], AluOpType.is_equal, 0.0, 0, 1).then_inc(sem.gr, 1)
    vsync()
    v.wait_ge(sem.ldi, 16)
    vdo(v.tensor_copy(T.idxf[0:16, :], T.idx32[0:16, :]))
    g.tensor.wait_ge(sem.gr, 1)
    g.tensor.wait_ge(sem.vs, nv[0])
    g.tensor.matmul(T.pidx[:, 0:8], T.rep[0:16, :], T.idxf[0:16, :], True, True).then_inc(sem.tm, 1)
    vsync()
    v.wait_ge(sem.tm, 1)
    vdo(v.tensor_copy(T.off[:], T.pidx[:, 0:8]))

    k1 = sched[rank][0][0]
    lot1 = list(range(LO[k1] // B, (LO[k1] + WID[k1] + B - 1) // B))
    lot2 = [b for b in range(M // B) if b not in lot1]

    def halves(lot):
        h = (len(lot) + 1) // 2
        return lot[:h], lot[h:]

    def take(lot):
        b0, b1 = lot[0], lot[-1] + 1
        return T.gat[:, b0 * B:b1 * B], T.xs[:, 0:TCOLS].indirect(T.off[:, b0 * OC:b1 * OC])

    g.scalar.wait_ge(sem.vs, nv[0])
    g.scalar.wait_ge(sem.ldx, 16)
    v.wait_ge(sem.ldx, 16)
    ready = []
    for lot, ss in ((lot1, sem.sg1), (lot2, sem.sg2)):
        lv, ls = halves(lot)
        o, i = take(ls)
        g.scalar.activation(o, i, ActivationFunctionType.Copy).then_inc(ss, 1)
        o, i = take(lv)
        vsync()
        vdo(v.tensor_copy(o, i))
        ready.append((nv[0], ss))

    sent = 0

    for gi, (k, dsts) in enumerate(sched[rank]):
        if gi < len(ready):
            g.wait_ge(sem.vs, ready[gi][0])
            g.wait_ge(ready[gi][1], 1)
        m = common_mask(rank, dsts)
        lands = []
        for d in dsts:
            t = place(rank, d)[1]
            lands.append(T.l1[:, t * WMAX:t * WMAX + WID[k]])
        g.remote_dma_fused([RemoteDMATransfer(
            dst_ids=[dst_id(d) for d in dsts], dma_engine_mask=m, remote_sem=sem["a1_%d_%d" % (gi, hb[rank])],
            srcs=[cols(T.gat, k)], dsts=lands, alu_op=0)], local_sem=sem.sent)
        sent += count(m)

    acc = T.acc[:, 0:w]
    inc = []
    for s in near[rank]:
        if s != rank:
            gi, t = place(s, rank)
            inc.append((t, gi, s))
    inc.sort()
    v.wait_ge(sem.sg1, 1)
    v.wait_ge(sem.sg2, 1)
    for n, (t, gi, s) in enumerate(inc):
        v.wait_ge(sem["a1_%d_%d" % (gi, hb[s])], count(common_mask(s, sched[s][gi][1])))
        land = T.l1[:, t * WMAX:t * WMAX + w]
        prev = cols(T.gat, a) if n == 0 else acc
        out = T.hs[:, 0:w] if n == len(inc) - 1 else acc
        vsync()
        vdo(v.tensor_tensor(out, land, prev, AluOpType.add))

    g.wait_ge(sem.vs, nv[0])
    m = topo.mask(core, cores[twin[rank]])
    g.remote_dma_fused([RemoteDMATransfer(
        dst_ids=[dst_id(twin[rank])], dma_engine_mask=m, remote_sem=sem.arr2,
        srcs=[T.hs[:, 0:w]], dsts=[T.l2[:, 0:w]], alu_op=0)], local_sem=sem.sent)
    sent += count(m)

    vsync()
    vdo(v.tensor_copy(acc, T.hs[:, 0:w]))
    v.wait_ge(sem.arr2, count(topo.mask(cores[twin[rank]], core)))
    vsync()
    vdo(v.tensor_tensor(cols(T.ys, a), T.l2[:, 0:w], acc, AluOpType.add))

    g.wait_ge(sem.vs, nv[0])
    m = common_mask(rank, others[rank])
    g.remote_dma_fused([RemoteDMATransfer(
        dst_ids=[dst_id(d) for d in others[rank]], dma_engine_mask=m, remote_sem=sem["a3_%d" % a],
        srcs=[cols(T.ys, a)], dsts=[cols(T.ys, a) for d in others[rank]], alu_op=0)],
        local_sem=sem.sent)
    sent += count(m)

    early = [s for s in others[rank] if others[s][0] == rank][0]
    late = [s for s in others[rank] if others[s][-1] == rank][0]
    g.scalar.wait_ge(sem.vs, nv[0])
    g.scalar.dma_start(cols(T.y, a), cols(T.ys, a)).then_inc(sem.st2, 16)
    g.scalar.wait_ge(sem["a3_%d" % pos[early]], count(common_mask(early, others[early])))
    g.scalar.dma_start(cols(T.y, pos[early]), cols(T.ys, pos[early])).then_inc(sem.st2, 16)
    g.sync.wait_ge(sem["a3_%d" % pos[late]], count(common_mask(late, others[late])))
    g.sync.dma_start(cols(T.y, pos[late]), cols(T.ys, pos[late])).then_inc(sem.st, 16)
    g.sync.wait_ge(sem.st, 16)
    g.scalar.wait_ge(sem.st2, 32)
    g.wait_ge(sem.sent, sent)
